import numpy as np, ml_dtypes
CORES = [10,34,74,98]
N = 4
import mx_ref
NC, G, MB = 512, 4, 1
C = np.float32(0.043)
BF = ml_dtypes.bfloat16
def cut(t, i, w=512):
    return t[:, w * i:w * i + w]
def tile(rs):
    return np.stack(rs, axis=2).reshape(128, -1).astype(BF)
def layer(w, X):
    out = []
    for i in range(G):
        for t in range(len(X)):
            p = mx_ref.matmul(mx_ref.quantize(cut(w, len(X) * i + t)), X[t])
            z = p if t == 0 else z + p
        out.append(z)
    return out
def act(Z):
    return [np.maximum(z, 0) * C for z in Z]
def setup_inputs(rng):
    def f(*shape):
        return mx_ref.flush((rng.standard_normal(shape, dtype=np.float32) * np.exp2(rng.integers(-2, 3, shape[:-1] + (1,)))).astype(BF))
    return {"x": f(N, 128, MB * 4 * NC), "w": f(N, 128, G * 512)}
def setup_inputs_blocks(rng):
    d = setup_inputs(rng)
    for k in ("x",): d[k] = mx_ref.spread(d[k], rng, 4)
    for k in ("w",): d[k] = mx_ref.spread(d[k], rng, 1)
    return d
def setup_inputs_wide(rng):
    d = setup_inputs(rng)
    for k in ("x",): d[k] = mx_ref.flush((d[k].astype(np.float32) * np.exp2(rng.integers(-8, 9, (N, 1, 1))).astype(np.float32)).astype(BF))
    return d
def setup_inputs_zeros(rng):
    d = setup_inputs(rng); v = d["x"].reshape(N, 128, -1, 4).copy()
    v[np.broadcast_to((rng.random((N, 1, v.shape[2], 1)) < 0.33), v.shape)] = 0
    d["x"] = v.reshape(d["x"].shape)
    return d
def reference(x, w):
    y = np.full((N, 128, MB * G * NC), np.nan, np.float32)
    for m in range(MB):
        a = mx_ref.quantize(cut(x[N - 1], m, 4 * NC))
        for s in range(N - 1):
            a = mx_ref.quantize(tile(act(layer(w[s], [a]))))
        Z = layer(w[N - 1], [a])
        for i in range(G):
            y[N - 1][:, NC * (G * m + i):NC * (G * m + i) + NC] = Z[i]
    return {"y": y}

@@ -1,0 +1,123 @@
+from concourse.mybir import dt, AluOpType, ActivationFunctionType
+
+G = 4
+TW = 128
+CH = [128, 128, 128, 128]
+OFF = [sum(CH[:c]) for c in range(len(CH))]
+K = len(CH)
+NC = sum(CH)
+C = 0.043
+
+SCRATCH = {
+    "xt": ("sbuf", [128, 4 * NC], "bfloat16"),
+    "wt": ("sbuf", [128, 4 * G * TW], "bfloat16"),
+    "h": ("sbuf", [128, 4 * NC], "bfloat16"),
+    "wc": ("sbuf", [128, G * TW], "float8_e4m3fn_x4"),
+    "wp": ("sbuf", [128, G * TW], "uint8"),
+    "qc": ("sbuf", [128, NC], "float8_e4m3fn_x4"),
+    "qp": ("sbuf", [128, NC], "uint8"),
+    "rc": ("sbuf", [128, NC], "float8_e4m3fn_x4"),
+    "rp": ("sbuf", [128, NC], "uint8"),
+    "o": ("sbuf", [128, G * NC], "float32"),
+    "ps": ("psum", [128, 8 * 512], "float32"),
+}
+SEMAPHORES = (["xl%d" % c for c in range(K)] + ["wl%d" % i for i in range(G)] + ["wq%d" % i for i in range(G)]
+              + ["qd%d" % c for c in range(K)] + ["arr%d" % c for c in range(K)] + ["act%d" % c for c in range(K)]
+              + ["mm%d_%d" % (c, i) for c in range(K) for i in range(G)]
+              + ["ev%d_%d" % (c, i) for c in range(K) for i in range(G)]
+              + ["sent", "st_sync", "st_scalar"])
+
+
+def rank_program(g, core, T, topo):
+    rank = T.rank_of(core)
+    if rank is None:
+        return
+    n = len(T.cores)
+    last = rank == n - 1
+    S = T.sem
+    v, sc, te = g.vector, g.scalar, g.tensor
+    dmaq = [g.sync, g.scalar]
+
+    dst = T.cores[(rank + 1) % n]
+    if not topo.may_write(core, dst):
+        raise ValueError("core %d may not write to core %d" % (core, dst))
+    rid, pid, _ = topo.addr(dst)
+    mask = topo.mask(core, dst)
+    ne = bin(mask).count("1")
+
+    if last:
+        for c in range(K):
+            a, b = 4 * OFF[c], 4 * (OFF[c] + CH[c])
+            dmaq[c % 2].dma_start(T.xt[:, a:b], T.x[:, a:b]).then_inc(S["xl%d" % c], 16)
+        for q in dmaq:
+            q.wait_ge(S.sent, 2 * K * ne)
+    for i in range(G):
+        a, b = 4 * TW * i, 4 * TW * (i + 1)
+        dmaq[i % 2].dma_start(T.wt[:, a:b], T.w[:, a:b]).then_inc(S["wl%d" % i], 16)
+
+    if last:
+        for c in range(K):
+            a, b = OFF[c], OFF[c] + CH[c]
+            v.wait_ge(S["xl%d" % c], 16)
+            v.quantize_mx(T.qc[:, a:b], T.qp[:, a:b], T.xt[:, 4 * a:4 * b]).then_inc(S["qd%d" % c], 1)
+    for i in range(G):
+        a, b = TW * i, TW * (i + 1)
+        v.wait_ge(S["wl%d" % i], 16)
+        v.quantize_mx(T.wc[:, a:b], T.wp[:, a:b], T.wt[:, 4 * a:4 * b]).then_inc(S["wq%d" % i], 1)
+
+    for c in range(K):
+        a, b = OFF[c], OFF[c] + CH[c]
+        te.wait_ge(S["arr%d" % c], 2 * ne)
+        if c >= 2 and not last:
+            te.wait_ge(S["act%d" % (c - 2)], G)
+        for i in range(G):
+            if c == 0:
+                te.wait_ge(S["wq%d" % i], 1)
+            if c >= 2 and last:
+                te.wait_ge(S["ev%d_%d" % (c - 2, i)], 1)
+            p = 512 * (G * (c % 2) + i)
+            te.matmul_mx(T.ps[:, p:p + CH[c]], T.wc[:, TW * i:TW * (i + 1)], T.wp[:, TW * i:TW * (i + 1)],
+                         T.rc[:, a:b], T.rp[:, a:b], True, True).then_inc(S["mm%d_%d" % (c, i)], 1)
+
+    for c in range(K):
+        a, b = OFF[c], OFF[c] + CH[c]
+        for i in range(G):
+            p = 512 * (G * (c % 2) + i)
+            z = T.ps[:, p:p + CH[c]]
+            mm = S["mm%d_%d" % (c, i)]
+            if not last:
+                out = T.h[:, 4 * a + i:4 * b:4]
+                if i % 2 == 0:
+                    sc.wait_ge(mm, 1)
+                    sc.activation(out, z, ActivationFunctionType.Relu, scale=C).then_inc(S["act%d" % c], 1)
+                else:
+                    v.wait_ge(mm, 1)
+                    v.tensor_scalar(out, z, 0.0, C, AluOpType.max, AluOpType.mult).then_inc(S["act%d" % c], 1)
+            else:
+                lo, hi = NC * i + a, NC * i + b
+                ev = S["ev%d_%d" % (c, i)]
+                if i % 2 == 0:
+                    sc.wait_ge(mm, 1)
+                    sc.activation(T.o[:, lo:hi], z, ActivationFunctionType.Copy).then_inc(ev, 1)
+                    sc.wait_ge(ev, 1)
+                    sc.dma_start(T.y[:, lo:hi], T.o[:, lo:hi]).then_inc(S.st_scalar, 16)
+                else:
+                    v.wait_ge(mm, 1)
+                    v.tensor_copy(T.o[:, lo:hi], z).then_inc(ev, 1)
+                    g.sync.wait_ge(ev, 1)
+                    g.sync.dma_start(T.y[:, lo:hi], T.o[:, lo:hi]).then_inc(S.st_sync, 16)
+        if not last:
+            v.wait_ge(S["act%d" % c], G)
+            v.quantize_mx(T.qc[:, a:b], T.qp[:, a:b], T.h[:, 4 * a:4 * b]).then_inc(S["qd%d" % c], 1)
+    if last:
+        sc.wait_ge(S.st_scalar, 16 * K * (G // 2))
+        g.sync.wait_ge(S.st_sync, 16 * K * (G // 2))
+
+    for c in range(K):
+        a, b = OFF[c], OFF[c] + CH[c]
+        g.wait_ge(S["qd%d" % c], 1)
+        g.remote_dma(out_ap=T.rc[:, a:b].bitcast(dt.uint8), in_ap=T.qc[:, a:b].bitcast(dt.uint8),
+                     remote_sem=S["arr%d" % c], local_sem=S.sent, pid=pid, routing_id=rid, dma_engine_mask=mask)
+        g.remote_dma(out_ap=T.rp[:, a:b], in_ap=T.qp[:, a:b],
+                     remote_sem=S["arr%d" % c], local_sem=S.sent, pid=pid, routing_id=rid, dma_engine_mask=mask)
+    g.wait_ge(S.sent, 2 * K * ne)

@@ -7,6 +7,8 @@ OFF = [sum(CH[:c]) for c in range(len(CH))]
 K = len(CH)
 NC = sum(CH)
 C = 0.043
+VIA = {2: 1, 3: 2}
+XORD = [0, 2, 3, 1]
 
 SCRATCH = {
     "xt": ("sbuf", [128, 4 * NC], "bfloat16"),
@@ -18,14 +20,15 @@ SCRATCH = {
     "qp": ("sbuf", [128, NC], "uint8"),
     "rc": ("sbuf", [128, NC], "float8_e4m3fn_x4"),
     "rp": ("sbuf", [128, NC], "uint8"),
+    "xp": ("sbuf", [128, 128], "uint8"),
     "o": ("sbuf", [128, G * NC], "float32"),
     "ps": ("psum", [128, 8 * 512], "float32"),
 }
-SEMAPHORES = (["xl%d" % c for c in range(K)] + ["wl%d" % i for i in range(G)] + ["wq%d" % i for i in range(G)]
+SEMAPHORES = (["xl%d" % c for c in range(K)] + ["wl%d" % i for i in range(G)] + ["wq"]
               + ["qd%d" % c for c in range(K)] + ["arr%d" % c for c in range(K)] + ["act%d" % c for c in range(K)]
               + ["mm%d_%d" % (c, i) for c in range(K) for i in range(G)]
               + ["ev%d_%d" % (c, i) for c in range(K) for i in range(G)]
-              + ["sent", "st_sync", "st_scalar"])
+              + ["sent", "st", "rel"])
 
 
 def rank_program(g, core, T, topo):
@@ -35,46 +38,47 @@ def rank_program(g, core, T, topo):
     n = len(T.cores)
     last = rank == n - 1
     S = T.sem
-    v, sc, te = g.vector, g.scalar, g.tensor
-    dmaq = [g.sync, g.scalar]
+    v, sc, te, sy = g.vector, g.scalar, g.tensor, g.sync
 
-    dst = T.cores[(rank + 1) % n]
-    if not topo.may_write(core, dst):
-        raise ValueError("core %d may not write to core %d" % (core, dst))
-    rid, pid, _ = topo.addr(dst)
-    mask = topo.mask(core, dst)
+    def way(to):
+        if not topo.may_write(core, to):
+            raise ValueError("core %d may not write to core %d" % (core, to))
+        r, p, _ = topo.addr(to)
+        return r, p, topo.mask(core, to)
+
+    rid, pid, mask = way(T.cores[(rank + 1) % n])
     ne = bin(mask).count("1")
 
     if last:
-        for c in range(K):
+        for k, c in enumerate(XORD):
             a, b = 4 * OFF[c], 4 * (OFF[c] + CH[c])
-            dmaq[c % 2].dma_start(T.xt[:, a:b], T.x[:, a:b]).then_inc(S["xl%d" % c], 16)
-        for q in dmaq:
-            q.wait_ge(S.sent, 2 * K * ne)
+            [sy, sc][k % 2].dma_start(T.xt[:, a:b], T.x[:, a:b]).then_inc(S["xl%d" % c], 16)
+        sy.wait_ge(S.sent, 2 * K * ne)
     for i in range(G):
         a, b = 4 * TW * i, 4 * TW * (i + 1)
-        dmaq[i % 2].dma_start(T.wt[:, a:b], T.w[:, a:b]).then_inc(S["wl%d" % i], 16)
+        (sy if last else [sy, sc][i % 2]).dma_start(T.wt[:, a:b], T.w[:, a:b]).then_inc(S["wl%d" % i], 16)
 
     if last:
-        for c in range(K):
+        for c in XORD:
             a, b = OFF[c], OFF[c] + CH[c]
             v.wait_ge(S["xl%d" % c], 16)
             v.quantize_mx(T.qc[:, a:b], T.qp[:, a:b], T.xt[:, 4 * a:4 * b]).then_inc(S["qd%d" % c], 1)
     for i in range(G):
         a, b = TW * i, TW * (i + 1)
         v.wait_ge(S["wl%d" % i], 16)
-        v.quantize_mx(T.wc[:, a:b], T.wp[:, a:b], T.wt[:, 4 * a:4 * b]).then_inc(S["wq%d" % i], 1)
+        v.quantize_mx(T.wc[:, a:b], T.wp[:, a:b], T.wt[:, 4 * a:4 * b]).then_inc(S.wq, 1)
 
+    te.wait_ge(S.wq, G)
     for c in range(K):
         a, b = OFF[c], OFF[c] + CH[c]
+        if c >= 2:
+            if last:
+                for i in range(G):
+                    te.wait_ge(S["ev%d_%d" % (c - 2, i)], 1)
+            else:
+                te.wait_ge(S["act%d" % (c - 2)], G)
         te.wait_ge(S["arr%d" % c], 2 * ne)
-        if c >= 2 and not last:
-            te.wait_ge(S["act%d" % (c - 2)], G)
         for i in range(G):
-            if c == 0:
-                te.wait_ge(S["wq%d" % i], 1)
-            if c >= 2 and last:
-                te.wait_ge(S["ev%d_%d" % (c - 2, i)], 1)
             p = 512 * (G * (c % 2) + i)
             te.matmul_mx(T.ps[:, p:p + CH[c]], T.wc[:, TW * i:TW * (i + 1)], T.wp[:, TW * i:TW * (i + 1)],
                          T.rc[:, a:b], T.rp[:, a:b], True, True).then_inc(S["mm%d_%d" % (c, i)], 1)
@@ -87,7 +91,7 @@ def rank_program(g, core, T, topo):
             mm = S["mm%d_%d" % (c, i)]
             if not last:
                 out = T.h[:, 4 * a + i:4 * b:4]
-                if i % 2 == 0:
+                if i < G - 1:
                     sc.wait_ge(mm, 1)
                     sc.activation(out, z, ActivationFunctionType.Relu, scale=C).then_inc(S["act%d" % c], 1)
                 else:
@@ -99,25 +103,58 @@ def rank_program(g, core, T, topo):
                 if i % 2 == 0:
                     sc.wait_ge(mm, 1)
                     sc.activation(T.o[:, lo:hi], z, ActivationFunctionType.Copy).then_inc(ev, 1)
-                    sc.wait_ge(ev, 1)
-                    sc.dma_start(T.y[:, lo:hi], T.o[:, lo:hi]).then_inc(S.st_scalar, 16)
                 else:
                     v.wait_ge(mm, 1)
                     v.tensor_copy(T.o[:, lo:hi], z).then_inc(ev, 1)
-                    g.sync.wait_ge(ev, 1)
-                    g.sync.dma_start(T.y[:, lo:hi], T.o[:, lo:hi]).then_inc(S.st_sync, 16)
+                sy.wait_ge(ev, 1)
+                sy.dma_start(T.y[:, lo:hi], T.o[:, lo:hi]).then_inc(S.st, 16)
         if not last:
             v.wait_ge(S["act%d" % c], G)
             v.quantize_mx(T.qc[:, a:b], T.qp[:, a:b], T.h[:, 4 * a:4 * b]).then_inc(S["qd%d" % c], 1)
     if last:
-        sc.wait_ge(S.st_scalar, 16 * K * (G // 2))
-        g.sync.wait_ge(S.st_sync, 16 * K * (G // 2))
+        sy.wait_ge(S.st, 16 * K * G)
 
-    for c in range(K):
+    def codes(c):
         a, b = OFF[c], OFF[c] + CH[c]
-        g.wait_ge(S["qd%d" % c], 1)
         g.remote_dma(out_ap=T.rc[:, a:b].bitcast(dt.uint8), in_ap=T.qc[:, a:b].bitcast(dt.uint8),
                      remote_sem=S["arr%d" % c], local_sem=S.sent, pid=pid, routing_id=rid, dma_engine_mask=mask)
+
+    def plane(c):
+        a, b = OFF[c], OFF[c] + CH[c]
         g.remote_dma(out_ap=T.rp[:, a:b], in_ap=T.qp[:, a:b],
                      remote_sem=S["arr%d" % c], local_sem=S.sent, pid=pid, routing_id=rid, dma_engine_mask=mask)
-    g.wait_ge(S.sent, 2 * K * ne)
+
+    calls = 2 * K
+    if last:
+        g.wait_ge(S.qd0, 1)
+        codes(0)
+        plane(0)
+        for c in sorted(VIA):
+            a, b = OFF[c], OFF[c] + CH[c]
+            mr, mp, mm_ = way(T.cores[VIA[c]])
+            if mm_ != mask:
+                raise ValueError("unlike masks")
+            g.wait_ge(S["qd%d" % c], 1)
+            g.remote_dma(out_ap=T.xp[:, 0:CH[c]], in_ap=T.qp[:, a:b], remote_sem=S.rel, local_sem=S.sent,
+                         pid=mp, routing_id=mr, dma_engine_mask=mask)
+        for c in range(1, K):
+            g.wait_ge(S["qd%d" % c], 1)
+            codes(c)
+            if c not in VIA:
+                plane(c)
+    else:
+        for c in sorted(VIA):
+            if VIA[c] == rank:
+                a, b = OFF[c], OFF[c] + CH[c]
+                er, ep, em = way(T.cores[0])
+                if em != mask:
+                    raise ValueError("unlike masks")
+                g.wait_ge(S.rel, ne)
+                g.remote_dma(out_ap=T.rp[:, a:b], in_ap=T.xp[:, 0:CH[c]], remote_sem=S["arr%d" % c], local_sem=S.sent,
+                             pid=ep, routing_id=er, dma_engine_mask=mask)
+                calls += 1
+        for c in range(K):
+            g.wait_ge(S["qd%d" % c], 1)
+            codes(c)
+            plane(c)
+    g.wait_ge(S.sent, calls * ne)

from concourse.mybir import dt, AluOpType, ActivationFunctionType

G = 4
TW = 128
CH = [128, 128, 128, 128]
OFF = [sum(CH[:c]) for c in range(len(CH))]
K = len(CH)
NC = sum(CH)
C = 0.043
VIA = {2: 1, 3: 2}
XORD = [0, 2, 3, 1]

SCRATCH = {
    "xt": ("sbuf", [128, 4 * NC], "bfloat16"),
    "wt": ("sbuf", [128, 4 * G * TW], "bfloat16"),
    "h": ("sbuf", [128, 4 * NC], "bfloat16"),
    "wc": ("sbuf", [128, G * TW], "float8_e4m3fn_x4"),
    "wp": ("sbuf", [128, G * TW], "uint8"),
    "qc": ("sbuf", [128, NC], "float8_e4m3fn_x4"),
    "qp": ("sbuf", [128, NC], "uint8"),
    "rc": ("sbuf", [128, NC], "float8_e4m3fn_x4"),
    "rp": ("sbuf", [128, NC], "uint8"),
    "xp": ("sbuf", [128, 128], "uint8"),
    "o": ("sbuf", [128, G * NC], "float32"),
    "ps": ("psum", [128, 8 * 512], "float32"),
}
SEMAPHORES = (["xl%d" % c for c in range(K)] + ["wl%d" % i for i in range(G)] + ["wq"]
              + ["qd%d" % c for c in range(K)] + ["arr%d" % c for c in range(K)] + ["act%d" % c for c in range(K)]
              + ["mm%d_%d" % (c, i) for c in range(K) for i in range(G)]
              + ["ev%d_%d" % (c, i) for c in range(K) for i in range(G)]
              + ["sent", "st", "rel"])


def rank_program(g, core, T, topo):
    rank = T.rank_of(core)
    if rank is None:
        return
    n = len(T.cores)
    last = rank == n - 1
    S = T.sem
    v, sc, te, sy = g.vector, g.scalar, g.tensor, g.sync

    def way(to):
        if not topo.may_write(core, to):
            raise ValueError("core %d may not write to core %d" % (core, to))
        r, p, _ = topo.addr(to)
        return r, p, topo.mask(core, to)

    rid, pid, mask = way(T.cores[(rank + 1) % n])
    ne = bin(mask).count("1")

    if last:
        for k, c in enumerate(XORD):
            a, b = 4 * OFF[c], 4 * (OFF[c] + CH[c])
            [sy, sc][k % 2].dma_start(T.xt[:, a:b], T.x[:, a:b]).then_inc(S["xl%d" % c], 16)
        sy.wait_ge(S.sent, 2 * K * ne)
    for i in range(G):
        a, b = 4 * TW * i, 4 * TW * (i + 1)
        (sy if last else [sy, sc][i % 2]).dma_start(T.wt[:, a:b], T.w[:, a:b]).then_inc(S["wl%d" % i], 16)

    if last:
        for c in XORD:
            a, b = OFF[c], OFF[c] + CH[c]
            v.wait_ge(S["xl%d" % c], 16)
            v.quantize_mx(T.qc[:, a:b], T.qp[:, a:b], T.xt[:, 4 * a:4 * b]).then_inc(S["qd%d" % c], 1)
    for i in range(G):
        a, b = TW * i, TW * (i + 1)
        v.wait_ge(S["wl%d" % i], 16)
        v.quantize_mx(T.wc[:, a:b], T.wp[:, a:b], T.wt[:, 4 * a:4 * b]).then_inc(S.wq, 1)

    te.wait_ge(S.wq, G)
    for c in range(K):
        a, b = OFF[c], OFF[c] + CH[c]
        if c >= 2:
            if last:
                for i in range(G):
                    te.wait_ge(S["ev%d_%d" % (c - 2, i)], 1)
            else:
                te.wait_ge(S["act%d" % (c - 2)], G)
        te.wait_ge(S["arr%d" % c], 2 * ne)
        for i in range(G):
            p = 512 * (G * (c % 2) + i)
            te.matmul_mx(T.ps[:, p:p + CH[c]], T.wc[:, TW * i:TW * (i + 1)], T.wp[:, TW * i:TW * (i + 1)],
                         T.rc[:, a:b], T.rp[:, a:b], True, True).then_inc(S["mm%d_%d" % (c, i)], 1)

    for c in range(K):
        a, b = OFF[c], OFF[c] + CH[c]
        for i in range(G):
            p = 512 * (G * (c % 2) + i)
            z = T.ps[:, p:p + CH[c]]
            mm = S["mm%d_%d" % (c, i)]
            if not last:
                out = T.h[:, 4 * a + i:4 * b:4]
                if i < G - 1:
                    sc.wait_ge(mm, 1)
                    sc.activation(out, z, ActivationFunctionType.Relu, scale=C).then_inc(S["act%d" % c], 1)
                else:
                    v.wait_ge(mm, 1)
                    v.tensor_scalar(out, z, 0.0, C, AluOpType.max, AluOpType.mult).then_inc(S["act%d" % c], 1)
            else:
                lo, hi = NC * i + a, NC * i + b
                ev = S["ev%d_%d" % (c, i)]
                if i % 2 == 0:
                    sc.wait_ge(mm, 1)
                    sc.activation(T.o[:, lo:hi], z, ActivationFunctionType.Copy).then_inc(ev, 1)
                else:
                    v.wait_ge(mm, 1)
                    v.tensor_copy(T.o[:, lo:hi], z).then_inc(ev, 1)
                sy.wait_ge(ev, 1)
                sy.dma_start(T.y[:, lo:hi], T.o[:, lo:hi]).then_inc(S.st, 16)
        if not last:
            v.wait_ge(S["act%d" % c], G)
            v.quantize_mx(T.qc[:, a:b], T.qp[:, a:b], T.h[:, 4 * a:4 * b]).then_inc(S["qd%d" % c], 1)
    if last:
        sy.wait_ge(S.st, 16 * K * G)

    def codes(c):
        a, b = OFF[c], OFF[c] + CH[c]
        g.remote_dma(out_ap=T.rc[:, a:b].bitcast(dt.uint8), in_ap=T.qc[:, a:b].bitcast(dt.uint8),
                     remote_sem=S["arr%d" % c], local_sem=S.sent, pid=pid, routing_id=rid, dma_engine_mask=mask)

    def plane(c):
        a, b = OFF[c], OFF[c] + CH[c]
        g.remote_dma(out_ap=T.rp[:, a:b], in_ap=T.qp[:, a:b],
                     remote_sem=S["arr%d" % c], local_sem=S.sent, pid=pid, routing_id=rid, dma_engine_mask=mask)

    calls = 2 * K
    if last:
        g.wait_ge(S.qd0, 1)
        codes(0)
        plane(0)
        for c in sorted(VIA):
            a, b = OFF[c], OFF[c] + CH[c]
            mr, mp, mm_ = way(T.cores[VIA[c]])
            if mm_ != mask:
                raise ValueError("unlike masks")
            g.wait_ge(S["qd%d" % c], 1)
            g.remote_dma(out_ap=T.xp[:, 0:CH[c]], in_ap=T.qp[:, a:b], remote_sem=S.rel, local_sem=S.sent,
                         pid=mp, routing_id=mr, dma_engine_mask=mask)
        for c in range(1, K):
            g.wait_ge(S["qd%d" % c], 1)
            codes(c)
            if c not in VIA:
                plane(c)
    else:
        for c in sorted(VIA):
            if VIA[c] == rank:
                a, b = OFF[c], OFF[c] + CH[c]
                er, ep, em = way(T.cores[0])
                if em != mask:
                    raise ValueError("unlike masks")
                g.wait_ge(S.rel, ne)
                g.remote_dma(out_ap=T.rp[:, a:b], in_ap=T.xp[:, 0:CH[c]], remote_sem=S["arr%d" % c], local_sem=S.sent,
                             pid=ep, routing_id=er, dma_engine_mask=mask)
                calls += 1
        for c in range(K):
            g.wait_ge(S["qd%d" % c], 1)
            codes(c)
            plane(c)
    g.wait_ge(S.sent, calls * ne)
